import numpy as np
import ml_dtypes


def mxq(x, axis, fmt="e4m3"):
    dtype, down = {"e4m3": (ml_dtypes.float8_e4m3fn, 7), "e5m2": (ml_dtypes.float8_e5m2, 14)}[fmt]
    v = np.moveaxis(np.asarray(x, np.float32).astype(ml_dtypes.bfloat16).astype(np.float64), axis, -1)
    blocks = v.reshape(v.shape[:-1] + (-1, 32))
    amax = np.abs(blocks).max(-1, keepdims=True)
    byte = np.maximum(np.where(amax > 0, np.frexp(amax)[1] - 1 + 127, 0) - down, 1)
    scale = np.exp2(byte - 127.0)
    codes = (blocks / scale).astype(np.float32).astype(dtype).astype(np.float64)
    return np.moveaxis((codes * scale).reshape(v.shape), -1, axis)


WIDE = False


def mx_kscale(k):
    if not WIDE:
        return np.ones(k)
    levels = np.array([10, -10, 5, -5, 0])
    if k % 512:
        return np.exp2(np.random.permutation(np.resize(levels, k // 32))).repeat(32)
    a = np.empty((k // 512, 16))
    for p in range(k // 512):
        a[p, :8] = np.random.permutation(np.resize(levels, 8))
        for g in range(8):
            far = levels[np.abs(levels - a[p, g]) >= 10]
            a[p, g + 8] = far[np.random.randint(len(far))]
    return np.exp2(a.ravel()).repeat(32)


def f64(x):
    return np.asarray(x).astype(np.float64)


def striped(idx):
    return np.tile(idx.reshape(-1, 16).T, (8, 1)).astype(np.uint16)


def unstriped(offs):
    return offs[:16].T.reshape(-1).astype(np.int64)


def striped8(idx):
    return np.concatenate([x.reshape(-1, 16).T for x in idx]).astype(np.uint16)


def runs(offs, k):
    lists = np.stack([offs[16 * r : 16 * r + 16].T.reshape(-1) for r in range(8)]).astype(np.int64)
    return lists[np.arange(k) % 512 // 64]


def pack_weight(w):
    k, n = w.shape
    w = f64(np.asarray(w, np.float32).astype(ml_dtypes.bfloat16)).reshape(k // 32, 32, n)
    amax = np.abs(w).max(1)
    byte = np.clip(np.where(amax > 0, np.frexp(amax)[1] - 1 + 127 - 7, 1), 1, 254)
    scaled = (w * np.exp2(127.0 - byte)[:, None, :]).reshape(k, n).astype(np.float32)
    words = np.ascontiguousarray(scaled.reshape(k // 512, 128, 4, n).transpose(0, 1, 3, 2)).astype(ml_dtypes.float8_e4m3fn).view(np.uint8)
    return words, np.ascontiguousarray(byte.astype(np.uint8).reshape(k // 512, 16, n))


def unpack_weight(words, scales):
    g, p, n, _ = words.shape
    vals = np.ascontiguousarray(words).view(ml_dtypes.float8_e4m3fn).astype(np.float64) * np.repeat(np.exp2(scales.astype(np.float64) - 127.0), 8, axis=1)[..., None]
    return vals.transpose(0, 1, 3, 2).reshape(g * 512, n)


K, T, S, N, G, H = 512, 2048, 512, 512, 2048, 512


def setup_inputs():
    n = np.random.standard_normal
    s = mx_kscale(K)[:, None]
    u = mx_kscale(S)
    packed_xT = pack_weight(n((K, T)) * s)
    packed_dT = pack_weight(n((K, G)) / s)
    return {
        "x_words": packed_xT[0],
        "x_scales": packed_xT[1],
        "d_words": packed_dT[0],
        "d_scales": packed_dT[1],
        "gn": (np.random.uniform(0.5, 1.5, (H, 1)) * u[:, None]).astype(np.float32),
        "w1": (n((H, N)) / np.sqrt(H) / u[:, None]).astype(np.float32),
        "tau": np.random.uniform(0.5, 1.2, (N, 1)).astype(np.float32),
        "offs": striped(np.random.permutation(T)[:S]),
        "kidx": striped8(np.random.randint(0, G, (8, H))),
        "n1": striped(np.random.randint(0, S, G)),
        "n2": striped(np.random.permutation(S)),
        "n3": striped(np.random.permutation(S)),
    }


def reference(x_words, x_scales, d_words, d_scales, gn, w1, tau, offs, kidx, n1, n2, n3):
    d_kidx = unpack_weight(d_words, d_scales)[np.arange(K)[:, None], runs(kidx, K)]
    xq = unpack_weight(x_words, x_scales)[:, unstriped(offs)]
    s = 0.0625 * (d_kidx.T @ xq)
    mb = s[:, unstriped(n1)]
    mx = mb.reshape(H, S, 4).max(axis=2)
    z = f64(gn) * (s - mx)
    h = mxq(f64(w1), 0, "e4m3").T @ mxq(z, 0, "e4m3")
    sz = np.abs(h)
    ea = np.exp(-1.0 * (f64(tau) * sz[:, unstriped(n2)]))
    return (h - h[:, unstriped(n3)]) * ea

@@ -1,0 +1,279 @@
+from contextlib import ExitStack
+
+import concourse.mybir as mybir
+
+F32 = mybir.dt.float32
+BF16 = mybir.dt.bfloat16
+I32 = mybir.dt.int32
+U32 = mybir.dt.uint32
+U16 = mybir.dt.uint16
+U8 = mybir.dt.uint8
+FP8X4 = mybir.dt.float8_e4m3fn_x4
+ALU = mybir.AluOpType
+ACT = mybir.ActivationFunctionType
+
+P = 128
+PACK = 4
+TABLE = 2048
+S = 512
+MEMBERS = 4
+LANES = 16
+SPARE = 32
+HALF = S // 2
+CHUNKS = (128, 128, 128, 64, 64)
+COPIED = 384
+FLOPS = 2 * 2 * 512 * 512 * 512
+
+
+def tile_picked_keygmaxdela_none_p_kernel(
+    tc, x_words, x_scales, d_words, d_scales, gn, w1, tau, offs, kidx, n1, n2, n3, out
+):
+    nc = tc.nc
+    with ExitStack() as ctx:
+        lists = ctx.enter_context(tc.tile_pool(name="lists", bufs=1))
+        sb = ctx.enter_context(tc.tile_pool(name="sb", bufs=1))
+        ps = ctx.enter_context(tc.psum_pool(name="ps", bufs=1))
+
+        kidx_t = lists.tile([P, S // LANES], U16, name="kidx_t")
+        offs_t = lists.tile([P, S // LANES], U16, name="offs_t")
+        n1_t = lists.tile([P, MEMBERS * S // LANES], U16, name="n1_t")
+        n2_t = lists.tile([P, S // LANES], U16, name="n2_t")
+        n3_t = lists.tile([P, S // LANES], U16, name="n3_t")
+
+        d_sc = sb.tile([P, TABLE], U8, name="d_sc", align_bytes=64)
+        x_sc = sb.tile([P, TABLE], U8, name="x_sc", align_bytes=64)
+        d_plane = sb.tile([P, S], U8, name="d_plane", align_bytes=64)
+        nc.vector.memset(d_plane[:].bitcast(I32), 0)
+        s_win = [sb.tile([P, S + SPARE], F32, name=f"s_win{t}") for t in range(PACK)]
+        for t in range(PACK):
+            nc.gpsimd.memset(s_win[t][:, S:], 0.0)
+
+        d_wd = sb.tile([P, TABLE], U32, name="d_wd", tag="d_wd_then_w1", align_bytes=64)
+        x_wd = sb.tile([P, TABLE], U32, name="x_wd", align_bytes=64)
+        gn_t = sb.tile([P, PACK], F32, name="gn_t")
+
+        nc.sync.dma_start(kidx_t[:], kidx)
+        nc.sync.dma_start(
+            d_sc[:].bitcast(I32), d_scales[0].bitcast(I32).unsqueeze(1).to_broadcast([16, 8, TABLE // 4])
+        )
+        nc.sync.dma_start(offs_t[:], offs)
+        for q in range(4):
+            nc.sync.dma_start(
+                x_sc[32 * q : 32 * q + 32, :].bitcast(I32),
+                x_scales[0][4 * q : 4 * q + 4, :].bitcast(I32).unsqueeze(0).to_broadcast([8, 4, TABLE // 4]),
+            )
+        nc.sync.dma_start(d_wd[:].bitcast(I32), d_words[0].rearrange("p n t -> p (n t)").bitcast(I32))
+        nc.sync.dma_start(x_wd[:].bitcast(I32), x_words[0].rearrange("p n t -> p (n t)").bitcast(I32))
+        nc.sync.dma_start(n1_t[:], n1)
+        nc.sync.dma_start(n2_t[:], n2)
+        nc.sync.dma_start(n3_t[:], n3)
+        nc.gpsimd.dma_start(gn_t[:], gn.rearrange("(p t) o -> p (t o)", t=PACK))
+
+        d_sc_g = sb.tile([P, S], U8, name="d_sc_g", align_bytes=64)
+        d_sc_dealt = sb.tile([P, S], U8, name="d_sc_dealt", tag="dealt_then_tau", align_bytes=64)
+        x_sc_g = sb.tile([P, S], U8, name="x_sc_g", align_bytes=64)
+        d_wd_g = sb.tile([P, S], U32, name="d_wd_g", align_bytes=64)
+        d_wd_dealt = sb.tile([P, S], U32, name="d_wd_dealt", tag="keys_then_w1", align_bytes=64)
+        x_wd_g = sb.tile([P, S], U32, name="x_wd_g", tag="queries_then_w1", align_bytes=64)
+
+        nc.vector.tensor_copy(d_sc_g[:], d_sc[:].indirect(kidx_t[:]))
+        nc.vector.tensor_copy(
+            d_sc_dealt[:].rearrange("p (t m) -> p t m", t=PACK),
+            d_sc_g[:].rearrange("p (m t) -> p t m", t=PACK),
+        )
+        for r in range(4):
+            nc.scalar.dma_start(d_plane[r:P:32, :].bitcast(I32), d_sc_dealt[8 * r : P : 32, :].bitcast(I32))
+        nc.vector.tensor_copy(x_sc_g[:], x_sc[:].indirect(offs_t[:]))
+        nc.vector.tensor_copy(d_wd_g[:], d_wd[:].indirect(kidx_t[:]))
+        nc.vector.tensor_copy(
+            d_wd_dealt[:].rearrange("p (t m) -> p t m", t=PACK),
+            d_wd_g[:].rearrange("p (m t) -> p t m", t=PACK),
+        )
+        for u in range(2):
+            nc.vector.tensor_copy(
+                x_wd_g[:, u * HALF : (u + 1) * HALF],
+                x_wd[:].indirect(offs_t[:, u * HALF // LANES : (u + 1) * HALF // LANES]),
+            )
+
+        w_raw = sb.tile([P, PACK, S], F32, name="w_raw", tag="d_wd_then_w1", align_bytes=64)
+        nc.sync.dma_start(w_raw[:], w1.rearrange("(p t) m -> p t m", t=PACK))
+        tau_t = sb.tile([P, PACK], F32, name="tau_t", tag="dealt_then_tau", align_bytes=64)
+        with nc.allow_non_contiguous_dma(reason="one value a row"):
+            nc.gpsimd.dma_start(tau_t[:], tau.rearrange("(b p) o -> p (b o)", p=P))
+        neg_tau = sb.tile([P, PACK], F32, name="neg_tau")
+        nc.gpsimd.tensor_scalar(neg_tau[:], tau_t[:], -1.0, 0.0, ALU.mult, ALU.add)
+
+        def scores(bank, t, cols):
+            keys = slice(t * P, (t + 1) * P)
+            nc.tensor.matmul_mx(
+                out=bank,
+                lhsT=d_wd_dealt[:, keys].bitcast(FP8X4),
+                lhsT_scale=d_plane[:, keys],
+                rhs=x_wd_g[:, cols].bitcast(FP8X4),
+                rhs_scale=x_sc_g[:, cols],
+                start=True,
+                stop=True,
+            )
+
+        for u in range(2):
+            cols = slice(u * HALF, (u + 1) * HALF)
+            s_half = ps.tile([P, HALF], F32, name=f"s_half{u}", tag=f"bank{PACK * u}")
+            scores(s_half[:], 0, cols)
+            nc.scalar.activation(s_win[0][:, cols], s_half[:], ACT.Copy, scale=0.0625)
+        for t in range(1, PACK):
+            s_ps = ps.tile([P, S], F32, name=f"s_ps{t}", tag=f"bank{t}")
+            scores(s_ps[:], t, slice(0, S))
+            nc.vector.tensor_scalar(s_win[t][:, :S], s_ps[:], 0.0625, None, ALU.mult)
+
+        starts = [sum(CHUNKS[:k]) for k in range(len(CHUNKS))]
+        last = len(CHUNKS) - 1
+        early = starts[last]
+
+        mb = {}
+        for k, n in enumerate(CHUNKS):
+            c0 = MEMBERS * starts[k] // LANES
+            for t in range(PACK):
+                mb[k, t] = sb.tile([P, MEMBERS * n], F32, name=f"mb{k}_{t}")
+                nc.scalar.activation(
+                    mb[k, t][:], s_win[t][:].indirect(n1_t[:, c0 : c0 + MEMBERS * n // LANES]), ACT.Copy
+                )
+
+        w_bf = [
+            sb.tile([P, HALF, PACK], BF16, name=f"w_bf{u}", tag=tag, align_bytes=64)
+            for u, tag in enumerate(("keys_then_w1", "queries_then_w1"))
+        ]
+        w_codes = sb.tile([P, S], U32, name="w_codes", align_bytes=64)
+        w_plane = sb.tile([P, S], U8, name="w_plane", align_bytes=64)
+        z_codes = sb.tile([P, S], U32, name="z_codes", align_bytes=64)
+        z_plane = sb.tile([P, S], U8, name="z_plane", align_bytes=64)
+        pair = {}
+        mx = {}
+        diff = {}
+        z_bf = [sb.tile([P, n, PACK], BF16, name=f"z_bf{k}", align_bytes=64) for k, n in enumerate(CHUNKS)]
+        h_win = [sb.tile([P, S], F32, name=f"h_win{b}") for b in range(PACK)]
+        h_own = [sb.tile([P, S], F32, name=f"h_own{b}") for b in range(PACK)]
+        sz = [sb.tile([P, S], F32, name=f"sz{b}") for b in range(PACK)]
+        h_ps = {}
+
+        def weave_w(half):
+            cols = slice(half * HALF, (half + 1) * HALF)
+            nc.vector.tensor_copy(
+                w_bf[half][:].rearrange("p (c i) t -> p c t i", i=4),
+                w_raw[:, :, cols].rearrange("p t (c i) -> p c t i", i=4),
+            )
+
+        def quantize_w(half):
+            cols = slice(half * HALF, (half + 1) * HALF)
+            nc.vector.quantize_mx(
+                out=w_codes[:, cols].bitcast(FP8X4),
+                scales=w_plane[:, cols],
+                in_=w_bf[half][:].rearrange("p m t -> p (m t)"),
+            )
+
+        def max_pairs(k, t):
+            members = mb[k, t][:].rearrange("p (j e) -> p j e", e=MEMBERS)
+            pair[k, t] = sb.tile([P, CHUNKS[k], 2], F32, name="pair", bufs=2)
+            nc.vector.tensor_tensor(pair[k, t][:], members[:, :, 0:2], members[:, :, 2:4], ALU.max)
+
+        def max_final(k, t):
+            mx[k, t] = sb.tile([P, CHUNKS[k]], F32, name="mx", bufs=2)
+            nc.vector.tensor_tensor(mx[k, t][:], pair[k, t][:, :, 0], pair[k, t][:, :, 1], ALU.max)
+
+        def subtract(k, t):
+            cols = slice(starts[k], starts[k] + CHUNKS[k])
+            if t == 0:
+                diff[k] = sb.tile([P, PACK, CHUNKS[k]], F32, name="diff", bufs=1)
+            nc.vector.tensor_tensor(diff[k][:, t, :], s_win[t][:, cols], mx[k, t][:], ALU.subtract)
+
+        def weigh(k):
+            n = CHUNKS[k]
+            nc.vector.tensor_tensor(
+                z_bf[k][:].rearrange("p (c i) t -> p c t i", i=2),
+                diff[k][:].rearrange("p t (c i) -> p c t i", i=2),
+                gn_t[:].unsqueeze(1).unsqueeze(3).to_broadcast([P, n // 2, PACK, 2]),
+                ALU.mult,
+            )
+
+        def quantize_z(k):
+            cols = slice(starts[k], starts[k] + CHUNKS[k])
+            nc.vector.quantize_mx(
+                out=z_codes[:, cols].bitcast(FP8X4),
+                scales=z_plane[:, cols],
+                in_=z_bf[k][:].rearrange("p j t -> p (j t)"),
+            )
+
+        def values(bank, b, cols):
+            rows = slice(b * P, (b + 1) * P)
+            nc.tensor.matmul_mx(
+                out=bank,
+                lhsT=w_codes[:, rows].bitcast(FP8X4),
+                lhsT_scale=w_plane[:, rows],
+                rhs=z_codes[:, cols].bitcast(FP8X4),
+                rhs_scale=z_plane[:, cols],
+                start=True,
+                stop=True,
+            )
+
+        def multiply(k):
+            quantize_z(k)
+            for b in range(PACK):
+                h_ps[k, b] = ps.tile(
+                    [P, CHUNKS[k]], F32, name=f"h_ps{k}_{b}", tag=f"bank{PACK * ((k + 1) % 2) + b}"
+                )
+                values(h_ps[k, b][:], b, slice(starts[k], starts[k] + CHUNKS[k]))
+
+        def copy_out(k, b):
+            cols = slice(starts[k], starts[k] + CHUNKS[k])
+            nc.vector.tensor_copy(h_win[b][:, cols], h_ps[k, b][:])
+            if starts[k] >= COPIED:
+                nc.vector.tensor_copy(h_own[b][:, cols], h_ps[k, b][:])
+            elif starts[k] + CHUNKS[k] == COPIED:
+                nc.sync.dma_start(h_own[b][:, :COPIED], h_win[b][:, :COPIED])
+
+        steps = len(CHUNKS) * PACK
+        extra = {2: [lambda: weave_w(0)], 3: [lambda: weave_w(1)], 4: [lambda: quantize_w(0), lambda: quantize_w(1)]}
+        for step in range(steps + 4):
+            k, phase = divmod(step - 6, PACK)
+            if 0 <= k and phase == 0:
+                weigh(k)
+            if 2 <= step < steps + 2:
+                subtract(*divmod(step - 2, PACK))
+            for work in extra.get(step, []):
+                work()
+            if 0 <= k:
+                if phase == 1:
+                    multiply(k)
+                elif phase > 1 and k < last:
+                    copy_out(k, 2 * (phase - 2))
+                    copy_out(k, 2 * (phase - 2) + 1)
+            if 1 <= step < steps + 1:
+                max_final(*divmod(step - 1, PACK))
+            if step < steps:
+                max_pairs(*divmod(step, PACK))
+
+        for b in range(PACK):
+            nc.scalar.activation(sz[b][:, :early], h_win[b][:, :early], ACT.Abs)
+        for b in range(PACK):
+            if b == 0:
+                copy_out(last, b)
+                nc.scalar.activation(sz[b][:, early:], h_ps[last, b][:], ACT.Abs)
+            else:
+                nc.scalar.activation(h_win[b][:, early:], h_ps[last, b][:], ACT.Copy)
+                nc.scalar.activation(h_own[b][:, early:], h_ps[last, b][:], ACT.Copy)
+                nc.scalar.activation(sz[b][:, early:], h_ps[last, b][:], ACT.Abs)
+            ea = [sb.tile([P, HALF], F32, name=f"ea{b}_{u}") for u in range(2)]
+            back = [sb.tile([P, HALF], F32, name=f"back{b}_{u}") for u in range(2)]
+            res = [sb.tile([P, HALF], F32, name=f"res{b}_{u}") for u in range(2)]
+            for u in range(2):
+                cols = slice(u * HALF, (u + 1) * HALF)
+                entries = slice(u * HALF // LANES, (u + 1) * HALF // LANES)
+                nc.scalar.activation(
+                    ea[u][:], sz[b][:].indirect(n2_t[:, entries]), ACT.Exp, scale=neg_tau[:, b : b + 1]
+                )
+                nc.vector.tensor_tensor(
+                    back[u][:], h_win[b][:].indirect(n3_t[:, entries]), h_own[b][:, cols], ALU.subtract
+                )
+            for u in range(2):
+                cols = slice(u * HALF, (u + 1) * HALF)
+                nc.vector.scalar_tensor_tensor(res[u][:], back[u][:], -1.0, ea[u][:], ALU.mult, ALU.mult)
+                nc.sync.dma_start(out[b * P : (b + 1) * P, cols], res[u][:])

@@ -20,8 +20,7 @@ MEMBERS = 4
 LANES = 16
 SPARE = 32
 HALF = S // 2
-CHUNKS = (128, 128, 128, 64, 64)
-COPIED = 384
+CHUNKS = (128, 128, 128, 128)
 FLOPS = 2 * 2 * 512 * 512 * 512
 
 
@@ -42,66 +41,55 @@ def tile_picked_keygmaxdela_none_p_kernel(
 
         d_sc = sb.tile([P, TABLE], U8, name="d_sc", align_bytes=64)
         x_sc = sb.tile([P, TABLE], U8, name="x_sc", align_bytes=64)
-        d_plane = sb.tile([P, S], U8, name="d_plane", align_bytes=64)
-        nc.vector.memset(d_plane[:].bitcast(I32), 0)
+        planes = sb.tile([P, 2 * S], U8, name="planes", align_bytes=64)
+        nc.vector.memset(d_sc[:].bitcast(I32), 0)
+        nc.gpsimd.memset(x_sc[:].bitcast(I32), 0)
+        nc.vector.memset(planes[:].bitcast(I32), 0)
         s_win = [sb.tile([P, S + SPARE], F32, name=f"s_win{t}") for t in range(PACK)]
-        for t in range(PACK):
-            nc.gpsimd.memset(s_win[t][:, S:], 0.0)
 
         d_wd = sb.tile([P, TABLE], U32, name="d_wd", tag="d_wd_then_w1", align_bytes=64)
         x_wd = sb.tile([P, TABLE], U32, name="x_wd", align_bytes=64)
-        gn_t = sb.tile([P, PACK], F32, name="gn_t")
 
-        nc.sync.dma_start(kidx_t[:], kidx)
-        nc.sync.dma_start(
-            d_sc[:].bitcast(I32), d_scales[0].bitcast(I32).unsqueeze(1).to_broadcast([16, 8, TABLE // 4])
-        )
-        nc.sync.dma_start(offs_t[:], offs)
-        for q in range(4):
-            nc.sync.dma_start(
-                x_sc[32 * q : 32 * q + 32, :].bitcast(I32),
-                x_scales[0][4 * q : 4 * q + 4, :].bitcast(I32).unsqueeze(0).to_broadcast([8, 4, TABLE // 4]),
-            )
+        for tile, table in ((kidx_t, kidx), (offs_t, offs), (n1_t, n1), (n2_t, n2), (n3_t, n3)):
+            nc.sync.dma_start(tile[:], table)
+        nc.sync.dma_start(d_sc[0:P:8, :].bitcast(I32), d_scales[0].bitcast(I32))
+        nc.sync.dma_start(x_sc[0:P:8, :].bitcast(I32), x_scales[0].bitcast(I32))
         nc.sync.dma_start(d_wd[:].bitcast(I32), d_words[0].rearrange("p n t -> p (n t)").bitcast(I32))
         nc.sync.dma_start(x_wd[:].bitcast(I32), x_words[0].rearrange("p n t -> p (n t)").bitcast(I32))
-        nc.sync.dma_start(n1_t[:], n1)
-        nc.sync.dma_start(n2_t[:], n2)
-        nc.sync.dma_start(n3_t[:], n3)
-        nc.gpsimd.dma_start(gn_t[:], gn.rearrange("(p t) o -> p (t o)", t=PACK))
 
-        d_sc_g = sb.tile([P, S], U8, name="d_sc_g", align_bytes=64)
-        d_sc_dealt = sb.tile([P, S], U8, name="d_sc_dealt", tag="dealt_then_tau", align_bytes=64)
-        x_sc_g = sb.tile([P, S], U8, name="x_sc_g", align_bytes=64)
+        gn_t = sb.tile([P, PACK], F32, name="gn_t")
+        nc.gpsimd.dma_start(gn_t[:], gn.rearrange("(p t) o -> p (t o)", t=PACK))
+        neg_gn = sb.tile([P, PACK], F32, name="neg_gn")
+        nc.gpsimd.tensor_scalar(neg_gn[:], gn_t[:], -1.0, 0.0, ALU.mult, ALU.add)
+
+        sc_g = sb.tile([P, 2 * S], U8, name="sc_g", align_bytes=64)
+        d_plane = sb.tile([P, S], U8, name="d_plane", align_bytes=64)
         d_wd_g = sb.tile([P, S], U32, name="d_wd_g", align_bytes=64)
         d_wd_dealt = sb.tile([P, S], U32, name="d_wd_dealt", tag="keys_then_w1", align_bytes=64)
         x_wd_g = sb.tile([P, S], U32, name="x_wd_g", tag="queries_then_w1", align_bytes=64)
 
-        nc.vector.tensor_copy(d_sc_g[:], d_sc[:].indirect(kidx_t[:]))
-        nc.vector.tensor_copy(
-            d_sc_dealt[:].rearrange("p (t m) -> p t m", t=PACK),
-            d_sc_g[:].rearrange("p (m t) -> p t m", t=PACK),
-        )
+        nc.vector.tensor_copy(sc_g[:, :S], d_sc[:].indirect(kidx_t[:]))
+        nc.vector.tensor_copy(sc_g[:, S:], x_sc[:].indirect(offs_t[:]))
         for r in range(4):
-            nc.scalar.dma_start(d_plane[r:P:32, :].bitcast(I32), d_sc_dealt[8 * r : P : 32, :].bitcast(I32))
-        nc.vector.tensor_copy(x_sc_g[:], x_sc[:].indirect(offs_t[:]))
+            nc.scalar.dma_start(planes[r:P:32, :].bitcast(I32), sc_g[8 * r : P : 32, :].bitcast(I32))
         nc.vector.tensor_copy(d_wd_g[:], d_wd[:].indirect(kidx_t[:]))
         nc.vector.tensor_copy(
-            d_wd_dealt[:].rearrange("p (t m) -> p t m", t=PACK),
-            d_wd_g[:].rearrange("p (m t) -> p t m", t=PACK),
+            d_wd_dealt[:].rearrange("p (t c i) -> p c t i", t=PACK, i=4),
+            d_wd_g[:].rearrange("p (c i t) -> p c t i", t=PACK, i=4),
         )
         for u in range(2):
             nc.vector.tensor_copy(
                 x_wd_g[:, u * HALF : (u + 1) * HALF],
                 x_wd[:].indirect(offs_t[:, u * HALF // LANES : (u + 1) * HALF // LANES]),
             )
+            if u == 0:
+                nc.vector.tensor_copy(
+                    d_plane[:].rearrange("p (t m) -> p t m", t=PACK),
+                    planes[:, :S].rearrange("p (m t) -> p t m", t=PACK),
+                )
 
         w_raw = sb.tile([P, PACK, S], F32, name="w_raw", tag="d_wd_then_w1", align_bytes=64)
         nc.sync.dma_start(w_raw[:], w1.rearrange("(p t) m -> p t m", t=PACK))
-        tau_t = sb.tile([P, PACK], F32, name="tau_t", tag="dealt_then_tau", align_bytes=64)
-        with nc.allow_non_contiguous_dma(reason="one value a row"):
-            nc.gpsimd.dma_start(tau_t[:], tau.rearrange("(b p) o -> p (b o)", p=P))
-        neg_tau = sb.tile([P, PACK], F32, name="neg_tau")
-        nc.gpsimd.tensor_scalar(neg_tau[:], tau_t[:], -1.0, 0.0, ALU.mult, ALU.add)
 
         def scores(bank, t, cols):
             keys = slice(t * P, (t + 1) * P)
@@ -110,7 +98,7 @@ def tile_picked_keygmaxdela_none_p_kernel(
                 lhsT=d_wd_dealt[:, keys].bitcast(FP8X4),
                 lhsT_scale=d_plane[:, keys],
                 rhs=x_wd_g[:, cols].bitcast(FP8X4),
-                rhs_scale=x_sc_g[:, cols],
+                rhs_scale=planes[:, S + cols.start : S + cols.stop],
                 start=True,
                 stop=True,
             )
@@ -129,14 +117,17 @@ def tile_picked_keygmaxdela_none_p_kernel(
         last = len(CHUNKS) - 1
         early = starts[last]
 
-        mb = {}
-        for k, n in enumerate(CHUNKS):
-            c0 = MEMBERS * starts[k] // LANES
-            for t in range(PACK):
-                mb[k, t] = sb.tile([P, MEMBERS * n], F32, name=f"mb{k}_{t}")
-                nc.scalar.activation(
-                    mb[k, t][:], s_win[t][:].indirect(n1_t[:, c0 : c0 + MEMBERS * n // LANES]), ACT.Copy
-                )
+        pieces = [(t, starts[k], starts[k] + n) for k, n in enumerate(CHUNKS) for t in range(PACK)]
+        mid = (early + S) // 2
+        pieces[-1:] = [(PACK - 1, early, mid), (PACK - 1, mid, S)]
+        mb = []
+        for u, (t, j0, j1) in enumerate(pieces):
+            mb.append(sb.tile([P, j1 - j0, MEMBERS], F32, name=f"mb{u}"))
+            nc.scalar.activation(
+                mb[u][:].rearrange("p j e -> p (j e)"),
+                s_win[t][:].indirect(n1_t[:, MEMBERS * j0 // LANES : MEMBERS * j1 // LANES]),
+                ACT.Copy,
+            )
 
         w_bf = [
             sb.tile([P, HALF, PACK], BF16, name=f"w_bf{u}", tag=tag, align_bytes=64)
@@ -148,11 +139,12 @@ def tile_picked_keygmaxdela_none_p_kernel(
         z_plane = sb.tile([P, S], U8, name="z_plane", align_bytes=64)
         pair = {}
         mx = {}
-        diff = {}
-        z_bf = [sb.tile([P, n, PACK], BF16, name=f"z_bf{k}", align_bytes=64) for k, n in enumerate(CHUNKS)]
-        h_win = [sb.tile([P, S], F32, name=f"h_win{b}") for b in range(PACK)]
-        h_own = [sb.tile([P, S], F32, name=f"h_own{b}") for b in range(PACK)]
-        sz = [sb.tile([P, S], F32, name=f"sz{b}") for b in range(PACK)]
+        s_gn = sb.tile([P, PACK, S], F32, name="s_gn")
+        z_rows = sb.tile([P, PACK, S], BF16, name="z_rows")
+        z_bf = sb.tile([P, S, PACK], BF16, name="z_bf", align_bytes=64)
+        h_win = [sb.tile([P, 2 * S], F32, name=f"h_win{b}") for b in range(PACK)]
+        h_own = sb.tile([P, PACK, S], F32, name="h_own")
+        sz = [sb.tile([P, 2 * S], F32, name=f"sz{b}") for b in range(PACK)]
         h_ps = {}
 
         def weave_w(half):
@@ -170,36 +162,38 @@ def tile_picked_keygmaxdela_none_p_kernel(
                 in_=w_bf[half][:].rearrange("p m t -> p (m t)"),
             )
 
-        def max_pairs(k, t):
-            members = mb[k, t][:].rearrange("p (j e) -> p j e", e=MEMBERS)
-            pair[k, t] = sb.tile([P, CHUNKS[k], 2], F32, name="pair", bufs=2)
-            nc.vector.tensor_tensor(pair[k, t][:], members[:, :, 0:2], members[:, :, 2:4], ALU.max)
+        def weigh_scores(t):
+            nc.vector.tensor_scalar(s_gn[:, t, :], s_win[t][:, :S], gn_t[:, t : t + 1], None, ALU.mult)
 
-        def max_final(k, t):
-            mx[k, t] = sb.tile([P, CHUNKS[k]], F32, name="mx", bufs=2)
-            nc.vector.tensor_tensor(mx[k, t][:], pair[k, t][:, :, 0], pair[k, t][:, :, 1], ALU.max)
+        def max_pairs(u):
+            pair[u] = sb.tile([P, CHUNKS[0], 2], F32, name="pair", bufs=2)
+            nc.vector.tensor_tensor(pair[u][:], mb[u][:, :, 0:2], mb[u][:, :, 2:4], ALU.max)
 
-        def subtract(k, t):
-            cols = slice(starts[k], starts[k] + CHUNKS[k])
-            if t == 0:
-                diff[k] = sb.tile([P, PACK, CHUNKS[k]], F32, name="diff", bufs=1)
-            nc.vector.tensor_tensor(diff[k][:, t, :], s_win[t][:, cols], mx[k, t][:], ALU.subtract)
+        def max_final(u):
+            mx[u] = sb.tile([P, CHUNKS[0]], F32, name="mx", bufs=2)
+            nc.vector.tensor_tensor(mx[u][:], pair[u][:, :, 0], pair[u][:, :, 1], ALU.max)
 
-        def weigh(k):
-            n = CHUNKS[k]
-            nc.vector.tensor_tensor(
-                z_bf[k][:].rearrange("p (c i) t -> p c t i", i=2),
-                diff[k][:].rearrange("p t (c i) -> p c t i", i=2),
-                gn_t[:].unsqueeze(1).unsqueeze(3).to_broadcast([P, n // 2, PACK, 2]),
-                ALU.mult,
+        def max_whole(u):
+            mx[u] = sb.tile([P, S - mid], F32, name="mx", bufs=2)
+            nc.vector.tensor_reduce(mx[u][:], mb[u][:], mybir.AxisListType.X, ALU.max)
+
+        def subtract(u):
+            t, j0, j1 = pieces[u]
+            nc.vector.scalar_tensor_tensor(
+                z_rows[:, t, j0:j1], mx[u][:], neg_gn[:, t : t + 1], s_gn[:, t, j0:j1], ALU.mult, ALU.add
             )
 
-        def quantize_z(k):
-            cols = slice(starts[k], starts[k] + CHUNKS[k])
+        def weave_z(j0, j1):
+            nc.vector.tensor_copy(
+                z_bf[:, j0:j1, :].rearrange("p (c i) t -> p c t i", i=4),
+                z_rows[:, :, j0:j1].rearrange("p t (c i) -> p c t i", i=4),
+            )
+
+        def quantize_z(j0, j1):
             nc.vector.quantize_mx(
-                out=z_codes[:, cols].bitcast(FP8X4),
-                scales=z_plane[:, cols],
-                in_=z_bf[k][:].rearrange("p j t -> p (j t)"),
+                out=z_codes[:, j0:j1].bitcast(FP8X4),
+                scales=z_plane[:, j0:j1],
+                in_=z_bf[:, j0:j1, :].rearrange("p j t -> p (j t)"),
             )
 
         def values(bank, b, cols):
@@ -215,65 +209,94 @@ def tile_picked_keygmaxdela_none_p_kernel(
             )
 
         def multiply(k):
-            quantize_z(k)
+            n = CHUNKS[k]
+            cols = slice(starts[k], starts[k] + n)
+            quantize_z(starts[k], starts[k] + n)
+            h_ps[k] = ps.tile([P, PACK, n], F32, name=f"h_ps{k}", tag=f"bank{PACK + k}")
             for b in range(PACK):
-                h_ps[k, b] = ps.tile(
-                    [P, CHUNKS[k]], F32, name=f"h_ps{k}_{b}", tag=f"bank{PACK * ((k + 1) % 2) + b}"
-                )
-                values(h_ps[k, b][:], b, slice(starts[k], starts[k] + CHUNKS[k]))
+                values(h_ps[k][:, b, :], b, cols)
 
-        def copy_out(k, b):
-            cols = slice(starts[k], starts[k] + CHUNKS[k])
-            nc.vector.tensor_copy(h_win[b][:, cols], h_ps[k, b][:])
-            if starts[k] >= COPIED:
-                nc.vector.tensor_copy(h_own[b][:, cols], h_ps[k, b][:])
-            elif starts[k] + CHUNKS[k] == COPIED:
-                nc.sync.dma_start(h_own[b][:, :COPIED], h_win[b][:, :COPIED])
+        def copy_out(k):
+            nc.vector.tensor_copy(h_own[:, :, starts[k] : starts[k] + CHUNKS[k]], h_ps[k][:])
 
-        steps = len(CHUNKS) * PACK
-        extra = {2: [lambda: weave_w(0)], 3: [lambda: weave_w(1)], 4: [lambda: quantize_w(0), lambda: quantize_w(1)]}
-        for step in range(steps + 4):
-            k, phase = divmod(step - 6, PACK)
-            if 0 <= k and phase == 0:
-                weigh(k)
-            if 2 <= step < steps + 2:
-                subtract(*divmod(step - 2, PACK))
-            for work in extra.get(step, []):
-                work()
-            if 0 <= k:
-                if phase == 1:
-                    multiply(k)
-                elif phase > 1 and k < last:
-                    copy_out(k, 2 * (phase - 2))
-                    copy_out(k, 2 * (phase - 2) + 1)
-            if 1 <= step < steps + 1:
-                max_final(*divmod(step - 1, PACK))
-            if step < steps:
-                max_pairs(*divmod(step, PACK))
+        def copy_windows(j0, j1):
+            for b in range(PACK):
+                nc.sync.dma_start(h_win[b][:, j0:j1], h_own[:, b, j0:j1])
+
+        whole = len(pieces) - 2
+        for step in range(whole + 1):
+            if step >= 2:
+                subtract(step - 2)
+            if step >= 1:
+                max_final(step - 1)
+            if step < PACK:
+                weigh_scores(step)
+            if step in (2, 3):
+                weave_w(step - 2)
+            if step == 4:
+                quantize_w(0)
+                quantize_w(1)
+            k, phase = divmod(step - 5, PACK)
+            if k >= 0 and phase == 0:
+                weave_z(starts[k], starts[k] + CHUNKS[k])
+            if k >= 0 and phase == 1:
+                multiply(k)
+            if k >= 0 and phase == 2:
+                copy_out(k)
+                if k > 0:
+                    copy_windows(starts[k] if k > 1 else 0, starts[k + 1])
+            if step < whole:
+                max_pairs(step)
+        max_whole(whole)
+        subtract(whole - 1)
+        subtract(whole)
+        max_whole(whole + 1)
+        weave_z(early, mid)
+        subtract(whole + 1)
+        quantize_z(early, mid)
+        weave_z(mid, S)
+        quantize_z(mid, S)
+        tau_t = sb.tile([P, PACK], F32, name="tau_t", tag="d_wd_then_w1", align_bytes=64)
+        with nc.allow_non_contiguous_dma(reason="one value a row"):
+            nc.sync.dma_start(tau_t[:], tau.rearrange("(b p) o -> p (b o)", p=P))
+        neg_tau = sb.tile([P, PACK], F32, name="neg_tau")
+        nc.gpsimd.tensor_scalar(neg_tau[:], tau_t[:], -1.0, 0.0, ALU.mult, ALU.add)
+        late = slice(early, S)
+        h_first = ps.tile([P, S - early], F32, name="h_first", tag="bank0")
+        h_rest = ps.tile([P, PACK - 1, S - early], F32, name="h_rest", tag="bank1")
+        values(h_first[:], 0, late)
+        for b in range(1, PACK):
+            values(h_rest[:, b - 1, :], b, late)
 
         for b in range(PACK):
-            nc.scalar.activation(sz[b][:, :early], h_win[b][:, :early], ACT.Abs)
-        for b in range(PACK):
-            if b == 0:
-                copy_out(last, b)
-                nc.scalar.activation(sz[b][:, early:], h_ps[last, b][:], ACT.Abs)
-            else:
-                nc.scalar.activation(h_win[b][:, early:], h_ps[last, b][:], ACT.Copy)
-                nc.scalar.activation(h_own[b][:, early:], h_ps[last, b][:], ACT.Copy)
-                nc.scalar.activation(sz[b][:, early:], h_ps[last, b][:], ACT.Abs)
-            ea = [sb.tile([P, HALF], F32, name=f"ea{b}_{u}") for u in range(2)]
-            back = [sb.tile([P, HALF], F32, name=f"back{b}_{u}") for u in range(2)]
-            res = [sb.tile([P, HALF], F32, name=f"res{b}_{u}") for u in range(2)]
-            for u in range(2):
-                cols = slice(u * HALF, (u + 1) * HALF)
-                entries = slice(u * HALF // LANES, (u + 1) * HALF // LANES)
-                nc.scalar.activation(
-                    ea[u][:], sz[b][:].indirect(n2_t[:, entries]), ACT.Exp, scale=neg_tau[:, b : b + 1]
-                )
-                nc.vector.tensor_tensor(
-                    back[u][:], h_win[b][:].indirect(n3_t[:, entries]), h_own[b][:, cols], ALU.subtract
-                )
-            for u in range(2):
-                cols = slice(u * HALF, (u + 1) * HALF)
-                nc.vector.scalar_tensor_tensor(res[u][:], back[u][:], -1.0, ea[u][:], ALU.mult, ALU.mult)
-                nc.sync.dma_start(out[b * P : (b + 1) * P, cols], res[u][:])
+            nc.scalar.activation(sz[b][:, :early], h_own[:, b, :early], ACT.Abs)
+        nc.vector.tensor_copy(h_win[0][:, late], h_first[:])
+        nc.scalar.activation(h_own[:, 0, late], h_first[:], ACT.Copy)
+        nc.scalar.activation(sz[0][:, late], h_first[:], ACT.Abs)
+        nc.scalar.activation(h_own[:, 1:, late], h_rest[:], ACT.Copy)
+        nc.scalar.activation(h_win[1][:, late], h_rest[:, 0, :], ACT.Copy)
+        for b in range(2, PACK):
+            nc.sync.dma_start(h_win[b][:, late], h_own[:, b, late])
+
+        ea = [sb.tile([P, S], F32, name=f"ea{b}") for b in range(PACK)]
+        back = [sb.tile([P, S], F32, name=f"back{b}") for b in range(PACK)]
+
+        def look_up(b):
+            if b > 0:
+                nc.scalar.activation(sz[b][:, late], h_rest[:, b - 1, :], ACT.Abs)
+            nc.scalar.activation(ea[b][:], sz[b][:].indirect(n2_t[:]), ACT.Exp, scale=neg_tau[:, b : b + 1])
+            nc.vector.tensor_tensor(back[b][:], h_win[b][:].indirect(n3_t[:]), h_own[:, b, :], ALU.subtract)
+
+        def finish(b):
+            parts = 2 if b == PACK - 1 else 1
+            for u in range(parts):
+                cols = slice(u * S // parts, (u + 1) * S // parts)
+                res = sb.tile([P, S // parts], F32, name=f"res{b}_{u}")
+                nc.vector.scalar_tensor_tensor(res[:], back[b][:, cols], -1.0, ea[b][:, cols], ALU.mult, ALU.mult)
+                nc.sync.dma_start(out[b * P : (b + 1) * P, cols], res[:])
+
+        look_up(0)
+        for b in range(1, PACK):
+            look_up(b)
+            finish(b - 1)
+        finish(PACK - 1)

@@ -18,9 +18,10 @@ TABLE = 2048
 S = 512
 MEMBERS = 4
 LANES = 16
-SPARE = 32
+SPARE = 544
+BANK = 512
 HALF = S // 2
-CHUNKS = (128, 128, 128, 128)
+CHUNKS = (256, 128, 128)
 FLOPS = 2 * 2 * 512 * 512 * 512
 
 
@@ -73,20 +74,30 @@ def tile_picked_keygmaxdela_none_p_kernel(
         for r in range(4):
             nc.scalar.dma_start(planes[r:P:32, :].bitcast(I32), sc_g[8 * r : P : 32, :].bitcast(I32))
         nc.vector.tensor_copy(d_wd_g[:], d_wd[:].indirect(kidx_t[:]))
-        nc.vector.tensor_copy(
-            d_wd_dealt[:].rearrange("p (t c i) -> p c t i", t=PACK, i=4),
-            d_wd_g[:].rearrange("p (c i t) -> p c t i", t=PACK, i=4),
-        )
-        for u in range(2):
+
+        def deal_words(t0, t1):
+            nc.vector.tensor_copy(
+                d_wd_dealt[:].rearrange("p (t c i) -> p c t i", t=PACK, i=4)[:, :, t0:t1, :],
+                d_wd_g[:].rearrange("p (c i t) -> p c t i", t=PACK, i=4)[:, :, t0:t1, :],
+            )
+
+        def deal_bytes(t0, t1):
+            nc.vector.tensor_copy(
+                d_plane[:].rearrange("p (t m) -> p t m", t=PACK)[:, t0:t1, :],
+                planes[:, :S].rearrange("p (m t) -> p t m", t=PACK)[:, t0:t1, :],
+            )
+
+        def gather_queries(u):
             nc.vector.tensor_copy(
                 x_wd_g[:, u * HALF : (u + 1) * HALF],
                 x_wd[:].indirect(offs_t[:, u * HALF // LANES : (u + 1) * HALF // LANES]),
             )
-            if u == 0:
-                nc.vector.tensor_copy(
-                    d_plane[:].rearrange("p (t m) -> p t m", t=PACK),
-                    planes[:, :S].rearrange("p (m t) -> p t m", t=PACK),
-                )
+
+        deal_words(0, PACK)
+        gather_queries(0)
+        deal_bytes(0, 1)
+        gather_queries(1)
+        deal_bytes(1, PACK)
 
         w_raw = sb.tile([P, PACK, S], F32, name="w_raw", tag="d_wd_then_w1", align_bytes=64)
         nc.sync.dma_start(w_raw[:], w1.rearrange("(p t) m -> p t m", t=PACK))
@@ -163,14 +174,14 @@ def tile_picked_keygmaxdela_none_p_kernel(
             )
 
         def weigh_scores(t):
-            nc.vector.tensor_scalar(s_gn[:, t, :], s_win[t][:, :S], gn_t[:, t : t + 1], None, ALU.mult)
+            nc.gpsimd.tensor_scalar(s_gn[:, t, :], s_win[t][:, :S], gn_t[:, t : t + 1], 0.0, ALU.mult, ALU.add)
 
         def max_pairs(u):
-            pair[u] = sb.tile([P, CHUNKS[0], 2], F32, name="pair", bufs=2)
+            pair[u] = sb.tile([P, pieces[u][2] - pieces[u][1], 2], F32, name="pair", bufs=2)
             nc.vector.tensor_tensor(pair[u][:], mb[u][:, :, 0:2], mb[u][:, :, 2:4], ALU.max)
 
         def max_final(u):
-            mx[u] = sb.tile([P, CHUNKS[0]], F32, name="mx", bufs=2)
+            mx[u] = sb.tile([P, pieces[u][2] - pieces[u][1]], F32, name="mx", bufs=2)
             nc.vector.tensor_tensor(mx[u][:], pair[u][:, :, 0], pair[u][:, :, 1], ALU.max)
 
         def max_whole(u):
@@ -211,17 +222,22 @@ def tile_picked_keygmaxdela_none_p_kernel(
         def multiply(k):
             n = CHUNKS[k]
             cols = slice(starts[k], starts[k] + n)
+            per_bank = BANK // n
             quantize_z(starts[k], starts[k] + n)
-            h_ps[k] = ps.tile([P, PACK, n], F32, name=f"h_ps{k}", tag=f"bank{PACK + k}")
-            for b in range(PACK):
-                values(h_ps[k][:, b, :], b, cols)
+            h_ps[k] = []
+            for g in range(PACK // per_bank):
+                bank = ps.tile([P, per_bank, n], F32, name=f"h_ps{k}_{g}", tag=f"bank{PACK + 2 * k + g}")
+                for b in range(per_bank):
+                    values(bank[:, b, :], g * per_bank + b, cols)
+                h_ps[k].append(bank)
 
         def copy_out(k):
-            nc.vector.tensor_copy(h_own[:, :, starts[k] : starts[k] + CHUNKS[k]], h_ps[k][:])
-
-        def copy_windows(j0, j1):
+            cols = slice(starts[k], starts[k] + CHUNKS[k])
+            per_bank = BANK // CHUNKS[k]
+            for g, bank in enumerate(h_ps[k]):
+                nc.vector.tensor_copy(h_own[:, g * per_bank : (g + 1) * per_bank, cols], bank[:])
             for b in range(PACK):
-                nc.sync.dma_start(h_win[b][:, j0:j1], h_own[:, b, j0:j1])
+                nc.sync.dma_start(h_win[b][:, cols], h_own[:, b, cols])
 
         whole = len(pieces) - 2
         for step in range(whole + 1):
@@ -231,20 +247,17 @@ def tile_picked_keygmaxdela_none_p_kernel(
                 max_final(step - 1)
             if step < PACK:
                 weigh_scores(step)
-            if step in (2, 3):
-                weave_w(step - 2)
-            if step == 4:
+            if step in (1, 2):
+                weave_w(step - 1)
+            if step == 3:
                 quantize_w(0)
                 quantize_w(1)
             k, phase = divmod(step - 5, PACK)
             if k >= 0 and phase == 0:
                 weave_z(starts[k], starts[k] + CHUNKS[k])
-            if k >= 0 and phase == 1:
                 multiply(k)
-            if k >= 0 and phase == 2:
+            if k == 0 and phase == 1:
                 copy_out(k)
-                if k > 0:
-                    copy_windows(starts[k] if k > 1 else 0, starts[k + 1])
             if step < whole:
                 max_pairs(step)
         max_whole(whole)
@@ -253,9 +266,8 @@ def tile_picked_keygmaxdela_none_p_kernel(
         max_whole(whole + 1)
         weave_z(early, mid)
         subtract(whole + 1)
-        quantize_z(early, mid)
         weave_z(mid, S)
-        quantize_z(mid, S)
+        quantize_z(early, S)
         tau_t = sb.tile([P, PACK], F32, name="tau_t", tag="d_wd_then_w1", align_bytes=64)
         with nc.allow_non_contiguous_dma(reason="one value a row"):
             nc.sync.dma_start(tau_t[:], tau.rearrange("(b p) o -> p (b o)", p=P))
@@ -268,10 +280,15 @@ def tile_picked_keygmaxdela_none_p_kernel(
         for b in range(1, PACK):
             values(h_rest[:, b - 1, :], b, late)
 
+        middle = slice(starts[1], early)
+        nc.scalar.activation(h_own[:, :, middle], h_ps[1][0][:], ACT.Copy)
+        nc.scalar.activation(h_win[0][:, middle], h_ps[1][0][:, 0, :], ACT.Copy)
+        for b in range(1, PACK):
+            nc.sync.dma_start(h_win[b][:, middle], h_own[:, b, middle])
         for b in range(PACK):
             nc.scalar.activation(sz[b][:, :early], h_own[:, b, :early], ACT.Abs)
         nc.vector.tensor_copy(h_win[0][:, late], h_first[:])
-        nc.scalar.activation(h_own[:, 0, late], h_first[:], ACT.Copy)
+        nc.vector.tensor_copy(h_own[:, 0, late], h_first[:])
         nc.scalar.activation(sz[0][:, late], h_first[:], ACT.Abs)
         nc.scalar.activation(h_own[:, 1:, late], h_rest[:], ACT.Copy)
         nc.scalar.activation(h_win[1][:, late], h_rest[:, 0, :], ACT.Copy)
@@ -288,7 +305,7 @@ def tile_picked_keygmaxdela_none_p_kernel(
             nc.vector.tensor_tensor(back[b][:], h_win[b][:].indirect(n3_t[:]), h_own[:, b, :], ALU.subtract)
 
         def finish(b):
-            parts = 2 if b == PACK - 1 else 1
+            parts = 2 if b >= PACK - 2 else 1
             for u in range(parts):
                 cols = slice(u * S // parts, (u + 1) * S // parts)
                 res = sb.tile([P, S // parts], F32, name=f"res{b}_{u}")

from contextlib import ExitStack

import concourse.mybir as mybir

F32 = mybir.dt.float32
BF16 = mybir.dt.bfloat16
I32 = mybir.dt.int32
U32 = mybir.dt.uint32
U16 = mybir.dt.uint16
U8 = mybir.dt.uint8
FP8X4 = mybir.dt.float8_e4m3fn_x4
ALU = mybir.AluOpType
ACT = mybir.ActivationFunctionType

P = 128
PACK = 4
TABLE = 2048
S = 512
MEMBERS = 4
LANES = 16
SPARE = 544
BANK = 512
HALF = S // 2
CHUNKS = (256, 128, 128)
FLOPS = 2 * 2 * 512 * 512 * 512


def tile_picked_keygmaxdela_none_p_kernel(
    tc, x_words, x_scales, d_words, d_scales, gn, w1, tau, offs, kidx, n1, n2, n3, out
):
    nc = tc.nc
    with ExitStack() as ctx:
        lists = ctx.enter_context(tc.tile_pool(name="lists", bufs=1))
        sb = ctx.enter_context(tc.tile_pool(name="sb", bufs=1))
        ps = ctx.enter_context(tc.psum_pool(name="ps", bufs=1))

        kidx_t = lists.tile([P, S // LANES], U16, name="kidx_t")
        offs_t = lists.tile([P, S // LANES], U16, name="offs_t")
        n1_t = lists.tile([P, MEMBERS * S // LANES], U16, name="n1_t")
        n2_t = lists.tile([P, S // LANES], U16, name="n2_t")
        n3_t = lists.tile([P, S // LANES], U16, name="n3_t")

        d_sc = sb.tile([P, TABLE], U8, name="d_sc", align_bytes=64)
        x_sc = sb.tile([P, TABLE], U8, name="x_sc", align_bytes=64)
        planes = sb.tile([P, 2 * S], U8, name="planes", align_bytes=64)
        nc.vector.memset(d_sc[:].bitcast(I32), 0)
        nc.gpsimd.memset(x_sc[:].bitcast(I32), 0)
        nc.vector.memset(planes[:].bitcast(I32), 0)
        s_win = [sb.tile([P, S + SPARE], F32, name=f"s_win{t}") for t in range(PACK)]

        d_wd = sb.tile([P, TABLE], U32, name="d_wd", tag="d_wd_then_w1", align_bytes=64)
        x_wd = sb.tile([P, TABLE], U32, name="x_wd", align_bytes=64)

        for tile, table in ((kidx_t, kidx), (offs_t, offs), (n1_t, n1), (n2_t, n2), (n3_t, n3)):
            nc.sync.dma_start(tile[:], table)
        nc.sync.dma_start(d_sc[0:P:8, :].bitcast(I32), d_scales[0].bitcast(I32))
        nc.sync.dma_start(x_sc[0:P:8, :].bitcast(I32), x_scales[0].bitcast(I32))
        nc.sync.dma_start(d_wd[:].bitcast(I32), d_words[0].rearrange("p n t -> p (n t)").bitcast(I32))
        nc.sync.dma_start(x_wd[:].bitcast(I32), x_words[0].rearrange("p n t -> p (n t)").bitcast(I32))

        gn_t = sb.tile([P, PACK], F32, name="gn_t")
        nc.gpsimd.dma_start(gn_t[:], gn.rearrange("(p t) o -> p (t o)", t=PACK))
        neg_gn = sb.tile([P, PACK], F32, name="neg_gn")
        nc.gpsimd.tensor_scalar(neg_gn[:], gn_t[:], -1.0, 0.0, ALU.mult, ALU.add)

        sc_g = sb.tile([P, 2 * S], U8, name="sc_g", align_bytes=64)
        d_plane = sb.tile([P, S], U8, name="d_plane", align_bytes=64)
        d_wd_g = sb.tile([P, S], U32, name="d_wd_g", align_bytes=64)
        d_wd_dealt = sb.tile([P, S], U32, name="d_wd_dealt", tag="keys_then_w1", align_bytes=64)
        x_wd_g = sb.tile([P, S], U32, name="x_wd_g", tag="queries_then_w1", align_bytes=64)

        nc.vector.tensor_copy(sc_g[:, :S], d_sc[:].indirect(kidx_t[:]))
        nc.vector.tensor_copy(sc_g[:, S:], x_sc[:].indirect(offs_t[:]))
        for r in range(4):
            nc.scalar.dma_start(planes[r:P:32, :].bitcast(I32), sc_g[8 * r : P : 32, :].bitcast(I32))
        nc.vector.tensor_copy(d_wd_g[:], d_wd[:].indirect(kidx_t[:]))

        def deal_words(t0, t1):
            nc.vector.tensor_copy(
                d_wd_dealt[:].rearrange("p (t c i) -> p c t i", t=PACK, i=4)[:, :, t0:t1, :],
                d_wd_g[:].rearrange("p (c i t) -> p c t i", t=PACK, i=4)[:, :, t0:t1, :],
            )

        def deal_bytes(t0, t1):
            nc.vector.tensor_copy(
                d_plane[:].rearrange("p (t m) -> p t m", t=PACK)[:, t0:t1, :],
                planes[:, :S].rearrange("p (m t) -> p t m", t=PACK)[:, t0:t1, :],
            )

        def gather_queries(u):
            nc.vector.tensor_copy(
                x_wd_g[:, u * HALF : (u + 1) * HALF],
                x_wd[:].indirect(offs_t[:, u * HALF // LANES : (u + 1) * HALF // LANES]),
            )

        deal_words(0, PACK)
        gather_queries(0)
        deal_bytes(0, 1)
        gather_queries(1)
        deal_bytes(1, PACK)

        w_raw = sb.tile([P, PACK, S], F32, name="w_raw", tag="d_wd_then_w1", align_bytes=64)
        nc.sync.dma_start(w_raw[:], w1.rearrange("(p t) m -> p t m", t=PACK))

        def scores(bank, t, cols):
            keys = slice(t * P, (t + 1) * P)
            nc.tensor.matmul_mx(
                out=bank,
                lhsT=d_wd_dealt[:, keys].bitcast(FP8X4),
                lhsT_scale=d_plane[:, keys],
                rhs=x_wd_g[:, cols].bitcast(FP8X4),
                rhs_scale=planes[:, S + cols.start : S + cols.stop],
                start=True,
                stop=True,
            )

        for u in range(2):
            cols = slice(u * HALF, (u + 1) * HALF)
            s_half = ps.tile([P, HALF], F32, name=f"s_half{u}", tag=f"bank{PACK * u}")
            scores(s_half[:], 0, cols)
            nc.scalar.activation(s_win[0][:, cols], s_half[:], ACT.Copy, scale=0.0625)
        for t in range(1, PACK):
            s_ps = ps.tile([P, S], F32, name=f"s_ps{t}", tag=f"bank{t}")
            scores(s_ps[:], t, slice(0, S))
            nc.vector.tensor_scalar(s_win[t][:, :S], s_ps[:], 0.0625, None, ALU.mult)

        starts = [sum(CHUNKS[:k]) for k in range(len(CHUNKS))]
        last = len(CHUNKS) - 1
        early = starts[last]

        pieces = [(t, starts[k], starts[k] + n) for k, n in enumerate(CHUNKS) for t in range(PACK)]
        mid = (early + S) // 2
        pieces[-1:] = [(PACK - 1, early, mid), (PACK - 1, mid, S)]
        mb = []
        for u, (t, j0, j1) in enumerate(pieces):
            mb.append(sb.tile([P, j1 - j0, MEMBERS], F32, name=f"mb{u}"))
            nc.scalar.activation(
                mb[u][:].rearrange("p j e -> p (j e)"),
                s_win[t][:].indirect(n1_t[:, MEMBERS * j0 // LANES : MEMBERS * j1 // LANES]),
                ACT.Copy,
            )

        w_bf = [
            sb.tile([P, HALF, PACK], BF16, name=f"w_bf{u}", tag=tag, align_bytes=64)
            for u, tag in enumerate(("keys_then_w1", "queries_then_w1"))
        ]
        w_codes = sb.tile([P, S], U32, name="w_codes", align_bytes=64)
        w_plane = sb.tile([P, S], U8, name="w_plane", align_bytes=64)
        z_codes = sb.tile([P, S], U32, name="z_codes", align_bytes=64)
        z_plane = sb.tile([P, S], U8, name="z_plane", align_bytes=64)
        pair = {}
        mx = {}
        s_gn = sb.tile([P, PACK, S], F32, name="s_gn")
        z_rows = sb.tile([P, PACK, S], BF16, name="z_rows")
        z_bf = sb.tile([P, S, PACK], BF16, name="z_bf", align_bytes=64)
        h_win = [sb.tile([P, 2 * S], F32, name=f"h_win{b}") for b in range(PACK)]
        h_own = sb.tile([P, PACK, S], F32, name="h_own")
        sz = [sb.tile([P, 2 * S], F32, name=f"sz{b}") for b in range(PACK)]
        h_ps = {}

        def weave_w(half):
            cols = slice(half * HALF, (half + 1) * HALF)
            nc.vector.tensor_copy(
                w_bf[half][:].rearrange("p (c i) t -> p c t i", i=4),
                w_raw[:, :, cols].rearrange("p t (c i) -> p c t i", i=4),
            )

        def quantize_w(half):
            cols = slice(half * HALF, (half + 1) * HALF)
            nc.vector.quantize_mx(
                out=w_codes[:, cols].bitcast(FP8X4),
                scales=w_plane[:, cols],
                in_=w_bf[half][:].rearrange("p m t -> p (m t)"),
            )

        def weigh_scores(t):
            nc.gpsimd.tensor_scalar(s_gn[:, t, :], s_win[t][:, :S], gn_t[:, t : t + 1], 0.0, ALU.mult, ALU.add)

        def max_pairs(u):
            pair[u] = sb.tile([P, pieces[u][2] - pieces[u][1], 2], F32, name="pair", bufs=2)
            nc.vector.tensor_tensor(pair[u][:], mb[u][:, :, 0:2], mb[u][:, :, 2:4], ALU.max)

        def max_final(u):
            mx[u] = sb.tile([P, pieces[u][2] - pieces[u][1]], F32, name="mx", bufs=2)
            nc.vector.tensor_tensor(mx[u][:], pair[u][:, :, 0], pair[u][:, :, 1], ALU.max)

        def max_whole(u):
            mx[u] = sb.tile([P, S - mid], F32, name="mx", bufs=2)
            nc.vector.tensor_reduce(mx[u][:], mb[u][:], mybir.AxisListType.X, ALU.max)

        def subtract(u):
            t, j0, j1 = pieces[u]
            nc.vector.scalar_tensor_tensor(
                z_rows[:, t, j0:j1], mx[u][:], neg_gn[:, t : t + 1], s_gn[:, t, j0:j1], ALU.mult, ALU.add
            )

        def weave_z(j0, j1):
            nc.vector.tensor_copy(
                z_bf[:, j0:j1, :].rearrange("p (c i) t -> p c t i", i=4),
                z_rows[:, :, j0:j1].rearrange("p t (c i) -> p c t i", i=4),
            )

        def quantize_z(j0, j1):
            nc.vector.quantize_mx(
                out=z_codes[:, j0:j1].bitcast(FP8X4),
                scales=z_plane[:, j0:j1],
                in_=z_bf[:, j0:j1, :].rearrange("p j t -> p (j t)"),
            )

        def values(bank, b, cols):
            rows = slice(b * P, (b + 1) * P)
            nc.tensor.matmul_mx(
                out=bank,
                lhsT=w_codes[:, rows].bitcast(FP8X4),
                lhsT_scale=w_plane[:, rows],
                rhs=z_codes[:, cols].bitcast(FP8X4),
                rhs_scale=z_plane[:, cols],
                start=True,
                stop=True,
            )

        def multiply(k):
            n = CHUNKS[k]
            cols = slice(starts[k], starts[k] + n)
            per_bank = BANK // n
            quantize_z(starts[k], starts[k] + n)
            h_ps[k] = []
            for g in range(PACK // per_bank):
                bank = ps.tile([P, per_bank, n], F32, name=f"h_ps{k}_{g}", tag=f"bank{PACK + 2 * k + g}")
                for b in range(per_bank):
                    values(bank[:, b, :], g * per_bank + b, cols)
                h_ps[k].append(bank)

        def copy_out(k):
            cols = slice(starts[k], starts[k] + CHUNKS[k])
            per_bank = BANK // CHUNKS[k]
            for g, bank in enumerate(h_ps[k]):
                nc.vector.tensor_copy(h_own[:, g * per_bank : (g + 1) * per_bank, cols], bank[:])
            for b in range(PACK):
                nc.sync.dma_start(h_win[b][:, cols], h_own[:, b, cols])

        whole = len(pieces) - 2
        for step in range(whole + 1):
            if step >= 2:
                subtract(step - 2)
            if step >= 1:
                max_final(step - 1)
            if step < PACK:
                weigh_scores(step)
            if step in (1, 2):
                weave_w(step - 1)
            if step == 3:
                quantize_w(0)
                quantize_w(1)
            k, phase = divmod(step - 5, PACK)
            if k >= 0 and phase == 0:
                weave_z(starts[k], starts[k] + CHUNKS[k])
                multiply(k)
            if k == 0 and phase == 1:
                copy_out(k)
            if step < whole:
                max_pairs(step)
        max_whole(whole)
        subtract(whole - 1)
        subtract(whole)
        max_whole(whole + 1)
        weave_z(early, mid)
        subtract(whole + 1)
        weave_z(mid, S)
        quantize_z(early, S)
        tau_t = sb.tile([P, PACK], F32, name="tau_t", tag="d_wd_then_w1", align_bytes=64)
        with nc.allow_non_contiguous_dma(reason="one value a row"):
            nc.sync.dma_start(tau_t[:], tau.rearrange("(b p) o -> p (b o)", p=P))
        neg_tau = sb.tile([P, PACK], F32, name="neg_tau")
        nc.gpsimd.tensor_scalar(neg_tau[:], tau_t[:], -1.0, 0.0, ALU.mult, ALU.add)
        late = slice(early, S)
        h_first = ps.tile([P, S - early], F32, name="h_first", tag="bank0")
        h_rest = ps.tile([P, PACK - 1, S - early], F32, name="h_rest", tag="bank1")
        values(h_first[:], 0, late)
        for b in range(1, PACK):
            values(h_rest[:, b - 1, :], b, late)

        middle = slice(starts[1], early)
        nc.scalar.activation(h_own[:, :, middle], h_ps[1][0][:], ACT.Copy)
        nc.scalar.activation(h_win[0][:, middle], h_ps[1][0][:, 0, :], ACT.Copy)
        for b in range(1, PACK):
            nc.sync.dma_start(h_win[b][:, middle], h_own[:, b, middle])
        for b in range(PACK):
            nc.scalar.activation(sz[b][:, :early], h_own[:, b, :early], ACT.Abs)
        nc.vector.tensor_copy(h_win[0][:, late], h_first[:])
        nc.vector.tensor_copy(h_own[:, 0, late], h_first[:])
        nc.scalar.activation(sz[0][:, late], h_first[:], ACT.Abs)
        nc.scalar.activation(h_own[:, 1:, late], h_rest[:], ACT.Copy)
        nc.scalar.activation(h_win[1][:, late], h_rest[:, 0, :], ACT.Copy)
        for b in range(2, PACK):
            nc.sync.dma_start(h_win[b][:, late], h_own[:, b, late])

        ea = [sb.tile([P, S], F32, name=f"ea{b}") for b in range(PACK)]
        back = [sb.tile([P, S], F32, name=f"back{b}") for b in range(PACK)]

        def look_up(b):
            if b > 0:
                nc.scalar.activation(sz[b][:, late], h_rest[:, b - 1, :], ACT.Abs)
            nc.scalar.activation(ea[b][:], sz[b][:].indirect(n2_t[:]), ACT.Exp, scale=neg_tau[:, b : b + 1])
            nc.vector.tensor_tensor(back[b][:], h_win[b][:].indirect(n3_t[:]), h_own[:, b, :], ALU.subtract)

        def finish(b):
            parts = 2 if b >= PACK - 2 else 1
            for u in range(parts):
                cols = slice(u * S // parts, (u + 1) * S // parts)
                res = sb.tile([P, S // parts], F32, name=f"res{b}_{u}")
                nc.vector.scalar_tensor_tensor(res[:], back[b][:, cols], -1.0, ea[b][:, cols], ALU.mult, ALU.mult)
                nc.sync.dma_start(out[b * P : (b + 1) * P, cols], res[:])

        look_up(0)
        for b in range(1, PACK):
            look_up(b)
            finish(b - 1)
        finish(PACK - 1)
